import numpy as np
import ml_dtypes

BF16 = ml_dtypes.bfloat16


def bf(x):
    return np.asarray(x, np.float32).astype(BF16)


def f32(x):
    return np.asarray(x, np.float32)


def f64(x):
    return np.asarray(x).astype(np.float64)


def striped(idx):
    return np.tile(idx.reshape(-1, 16).T, (8, 1))


S, K, M, N = 256, 256, 128, 64


def setup_inputs():
    return {"base": bf(np.random.standard_normal((M, S))), "x": bf(np.random.standard_normal((K, N))), "w": bf(np.random.standard_normal((K, M)) / np.sqrt(K)), "b": f32(0.5 * np.random.standard_normal((M, 1))), "offs": striped(np.random.permutation(S)[:N])}


def reference(base, x, w, b, offs):
    idx = offs[:16].T.reshape(-1)
    z = f64(base).copy()
    z[:, idx] += f64(w).T @ f64(x)
    return z + f64(b)

import concourse.mybir as mybir
from concourse.masks import make_identity

P = 128
S = 256
K = 256
N = 64
BLOCKS = K // P

BF16, F32, U16 = mybir.dt.bfloat16, mybir.dt.float32, mybir.dt.uint16

FLOPS = 2 * K * P * N + 2 * P * S


def tile_scatter_matmul_kernel(tc, base, x, w, b, offs, out):
    nc = tc.nc
    with (
        tc.tile_pool(name="held", bufs=1) as held,
        tc.psum_pool(name="psum", bufs=1) as psum,
    ):
        base_tile = held.tile([P, S], BF16)
        w_tile = held.tile([P, BLOCKS, P], BF16)
        x_tile = held.tile([P, BLOCKS, N], BF16)
        offsets = held.tile([P, N // 16], U16)
        bias = held.tile([P, 1], F32)
        result = held.tile([P, S], F32)
        ident = held.tile([P, P], BF16)
        window = psum.tile([P, S], F32)

        nc.sync.dma_start(base_tile[:], base)
        nc.sync.dma_start(w_tile[:], w.rearrange("(p a) m -> p a m", a=BLOCKS))
        nc.sync.dma_start(x_tile[:], x.rearrange("(p a) n -> p a n", a=BLOCKS))
        nc.sync.dma_start(offsets[:], offs)
        nc.sync.dma_start(bias[:], b)
        make_identity(nc, ident[:])

        nc.tensor.matmul(window[:], ident[:], base_tile[:], start=True, stop=False)
        for a in range(BLOCKS):
            nc.tensor.matmul(
                window[:].indirect(offsets[:]), w_tile[:, a, :], x_tile[:, a, :], start=False, stop=a == BLOCKS - 1
            )

        nc.vector.tensor_scalar_add(result[:], window[:], bias[:, 0:1])
        nc.sync.dma_start(out, result[:])
